import numpy as np
import ml_dtypes


def mxq(x, axis, fmt="e4m3"):
    dtype, down = {"e4m3": (ml_dtypes.float8_e4m3fn, 7), "e5m2": (ml_dtypes.float8_e5m2, 14)}[fmt]
    v = np.moveaxis(np.asarray(x, np.float32).astype(ml_dtypes.bfloat16).astype(np.float64), axis, -1)
    blocks = v.reshape(v.shape[:-1] + (-1, 32))
    amax = np.abs(blocks).max(-1, keepdims=True)
    byte = np.maximum(np.where(amax > 0, np.frexp(amax)[1] - 1 + 127, 0) - down, 1)
    scale = np.exp2(byte - 127.0)
    codes = (blocks / scale).astype(np.float32).astype(dtype).astype(np.float64)
    return np.moveaxis((codes * scale).reshape(v.shape), -1, axis)


WIDE = False


def mx_kscale(k):
    if not WIDE:
        return np.ones(k)
    levels = np.array([10, -10, 5, -5, 0])
    if k % 512:
        return np.exp2(np.random.permutation(np.resize(levels, k // 32))).repeat(32)
    a = np.empty((k // 512, 16))
    for p in range(k // 512):
        a[p, :8] = np.random.permutation(np.resize(levels, 8))
        for g in range(8):
            far = levels[np.abs(levels - a[p, g]) >= 10]
            a[p, g + 8] = far[np.random.randint(len(far))]
    return np.exp2(a.ravel()).repeat(32)


def f64(x):
    return np.asarray(x).astype(np.float64)


def striped8(idx):
    return np.asarray(idx).reshape(8, -1, 16).transpose(0, 2, 1).reshape(128, -1).astype(np.uint16)


def unstriped8(offs):
    return offs.reshape(8, 16, -1).transpose(0, 2, 1).reshape(8, -1).astype(np.int64)


def pick8(x, idx, run):
    r = np.arange(len(x))
    return x[r[:, None], idx[r % (8 * run) // run]]


E2M1 = np.array([0.0, 0.5, 1.0, 1.5, 2.0, 3.0, 4.0, 6.0, -0.0, -0.5, -1.0, -1.5, -2.0, -3.0, -4.0, -6.0])


def pack_weight(w, fmt):
    k, n = w.shape
    w = f64(np.asarray(w, np.float32).astype(ml_dtypes.bfloat16)).reshape(k // 32, 32, n)
    amax = np.abs(w).max(1)
    if fmt == "e4m3":
        byte = np.frexp(amax)[1] - 1 + 127 - 7
    else:
        mant, ex = np.frexp(amax / 6.0)
        byte = np.where(mant > 0.5, ex, ex - 1) + 127
    byte = np.clip(np.where(amax > 0, byte, 1), 1, 254)
    scaled = (w * np.exp2(127.0 - byte)[:, None, :]).reshape(k, n).astype(np.float32)
    by_word = np.ascontiguousarray(scaled.reshape(k // 512, 128, 4, n).transpose(0, 1, 3, 2))
    if fmt == "e4m3":
        words = by_word.astype(ml_dtypes.float8_e4m3fn).view(np.uint8)
    else:
        c = by_word.astype(ml_dtypes.float4_e2m1fn).view(np.uint8) & 0xF
        words = (c[..., 0::2] | (c[..., 1::2] << 4)).reshape(k // 512, 128, 2 * n)
    return np.ascontiguousarray(words), np.ascontiguousarray(byte.astype(np.uint8).reshape(k // 512, 16, n))


def unpack_weight(words, scales, fmt):
    g, _, n = scales.shape
    words = np.ascontiguousarray(words).reshape(g, 128, n, -1)
    if fmt == "e4m3":
        vals = words.view(ml_dtypes.float8_e4m3fn).astype(np.float64)
    else:
        nib = np.empty((g, 128, n, 4), np.uint8)
        nib[..., 0::2] = words & 0xF
        nib[..., 1::2] = words >> 4
        vals = E2M1[nib]
    vals = vals * np.repeat(np.exp2(scales.astype(np.float64) - 127.0), 8, axis=1)[..., None]
    return vals.transpose(0, 1, 3, 2).reshape(g * 512, n)


D, T, I, Q = 512, 1024, 512, 128


def setup_inputs():
    n = np.random.standard_normal
    idx = np.stack([np.random.permutation(T)[:I] for _ in range(8)])
    idx2 = np.stack([np.random.permutation(T)[:I] for _ in range(8)])
    idx3 = np.stack([np.random.permutation(T)[:I] for _ in range(8)])
    fd = mx_kscale(D)
    keysp = pack_weight(n((D, T)) / fd[:, None], "e2m1")
    return {
        "query": (n((D, Q)) * 1.0 / np.sqrt(D) * fd[:, None]).astype(np.float32),
        "keys_words": keysp[0],
        "keys_scales": keysp[1],
        "old": (1.0 * n((Q, T))).astype(np.float32),
        "offs": striped8(idx),
        "offs2": striped8(idx2),
        "offs3": striped8(idx3),
    }


def reference(query, keys_words, keys_scales, old, offs, offs2, offs3):
    idx = unstriped8(offs)
    idx2 = unstriped8(offs2)
    idx3 = unstriped8(offs3)
    keysu = unpack_weight(keys_words, keys_scales, "e2m1")
    queryq = mxq(f64(query), 0, "e4m3")
    a = queryq.T @ keysu
    w = pick8(a, idx, 16) * pick8(a, idx2, 16)
    f1 = np.zeros((Q, T))
    f1[np.arange(Q)[:, None], idx3[np.arange(Q) % 128 // 16]] = w
    y = np.maximum(f1, f64(old)) + f64(old) * 0.25
    return y

@@ -1,0 +1,103 @@
+from contextlib import ExitStack
+
+import concourse.mybir as mybir
+
+D, T, I, Q = 512, 1024, 512, 128
+FLOPS = 2 * D * T * Q
+
+F32 = mybir.dt.float32
+BF16 = mybir.dt.bfloat16
+I32 = mybir.dt.int32
+U32 = mybir.dt.uint32
+U16 = mybir.dt.uint16
+U8 = mybir.dt.uint8
+FP8X4 = mybir.dt.float8_e4m3fn_x4
+FP4X4 = mybir.dt.float4_e2m1fn_x4
+ALU = mybir.AluOpType
+COPY = mybir.ActivationFunctionType.Copy
+
+P = 128
+SCORE_WIDTHS = (256, 256, 256, 128, 128)
+HALF = I // 2
+OUT_CHUNK = 256
+
+
+def tile_attend_pairproduct_lean_largerput_heads_kernel(tc, query, keys_words, keys_scales, old, offs, offs2, offs3, out):
+    nc = tc.nc
+    with ExitStack() as ctx:
+        lists = ctx.enter_context(tc.tile_pool(name="lists", bufs=1))
+        sb = ctx.enter_context(tc.tile_pool(name="sb", bufs=1))
+        psum = ctx.enter_context(tc.psum_pool(name="psum", bufs=1))
+
+        key_scales = sb.tile([P, T], U8, align_bytes=64)
+        nc.vector.memset(key_scales[:].bitcast(I32), 0)
+        placed = sb.tile([P, T], F32)
+        nc.vector.memset(placed[:], 0.0)
+
+        q_raw = sb.tile([P, 4, Q], F32, tag="stage")
+        nc.sync.dma_start(q_raw[:], query.rearrange("(p j) q -> p j q", j=4))
+        key_words = sb.tile([P, 2 * T], U8, align_bytes=64)
+        nc.sync.dma_start(key_words[:], keys_words[0])
+        for quad in range(4):
+            nc.sync.dma_start(
+                key_scales[32 * quad : 32 * quad + 4, :].bitcast(I32),
+                keys_scales[0, 4 * quad : 4 * quad + 4, :].bitcast(I32),
+            )
+        list1 = lists.tile([P, I // 16], U16)
+        nc.sync.dma_start(list1[:], offs)
+        list2 = lists.tile([P, I // 16], U16)
+        nc.sync.dma_start(list2[:], offs2)
+        list3 = lists.tile([P, I // 16], U16)
+        nc.sync.dma_start(list3[:], offs3)
+
+        q_bf = sb.tile([P, Q, 4], BF16, align_bytes=64)
+        nc.vector.tensor_copy(q_bf[:], q_raw[:].rearrange("p j q -> p q j"))
+        q_codes = sb.tile([P, Q], U32, align_bytes=64)
+        q_scales = sb.tile([P, Q], U8, align_bytes=64)
+        nc.vector.quantize_mx(q_codes[:].bitcast(FP8X4), q_scales[:], q_bf[:].rearrange("p q j -> p (q j)"))
+
+        old_sb = sb.tile([P, T], F32, tag="stage")
+        nc.sync.dma_start(old_sb[:], old)
+
+        scores = sb.tile([P, T], F32)
+        t0 = 0
+        for n, width in enumerate(SCORE_WIDTHS):
+            bank = psum.tile([P, width], F32, name=f"bank{n}")
+            nc.tensor.matmul_mx(
+                bank[:],
+                lhsT=q_codes[:].bitcast(FP8X4),
+                lhsT_scale=q_scales[:],
+                rhs=key_words[:, 2 * t0 : 2 * (t0 + width)].bitcast(FP4X4),
+                rhs_scale=key_scales[:, t0 : t0 + width],
+                start=True,
+                stop=True,
+            )
+            if n % 2 == 0:
+                nc.scalar.activation(scores[:, t0 : t0 + width], bank[:], COPY)
+            else:
+                nc.vector.tensor_copy(scores[:, t0 : t0 + width], bank[:])
+            t0 = t0 + width
+
+        for h in range(2):
+            cols = slice(h * HALF // 16, (h + 1) * HALF // 16)
+            first = sb.tile([P, HALF], F32, name=f"first{h}")
+            second = sb.tile([P, HALF], F32, name=f"second{h}")
+            if h == 0:
+                nc.vector.tensor_copy(first[:], scores[:].indirect(list1[:, cols]))
+            else:
+                nc.scalar.activation(first[:], scores[:].indirect(list1[:, cols]), COPY)
+            nc.scalar.activation(second[:], scores[:].indirect(list2[:, cols]), COPY)
+            nc.vector.tensor_tensor(placed[:].indirect(list3[:, cols]), first[:], second[:], ALU.mult)
+
+        chunks = T // OUT_CHUNK
+        larger = [sb.tile([P, OUT_CHUNK], F32, name=f"larger{c}") for c in range(chunks)]
+        result = [sb.tile([P, OUT_CHUNK], F32, name=f"result{c}") for c in range(chunks)]
+        for step in range(chunks + 1):
+            if step < chunks:
+                cols = slice(step * OUT_CHUNK, (step + 1) * OUT_CHUNK)
+                nc.vector.tensor_tensor(larger[step][:], placed[:, cols], old_sb[:, cols], ALU.max)
+            if step > 0:
+                c = step - 1
+                cols = slice(c * OUT_CHUNK, (c + 1) * OUT_CHUNK)
+                nc.vector.scalar_tensor_tensor(result[c][:], old_sb[:, cols], 0.25, larger[c][:], ALU.mult, ALU.add)
+                nc.sync.dma_start(out[:, cols], result[c][:])

@@ -1,6 +1,7 @@
 from contextlib import ExitStack
 
 import concourse.mybir as mybir
+from concourse.masks import make_identity
 
 D, T, I, Q = 512, 1024, 512, 128
 FLOPS = 2 * D * T * Q
@@ -18,8 +19,9 @@ COPY = mybir.ActivationFunctionType.Copy
 
 P = 128
 SCORE_WIDTHS = (256, 256, 256, 128, 128)
+WORDS_FIRST = 512
 HALF = I // 2
-OUT_CHUNK = 256
+SPLIT = 640
 
 
 def tile_attend_pairproduct_lean_largerput_heads_kernel(tc, query, keys_words, keys_scales, old, offs, offs2, offs3, out):
@@ -34,15 +36,19 @@ def tile_attend_pairproduct_lean_largerput_heads_kernel(tc, query, keys_words, k
         placed = sb.tile([P, T], F32)
         nc.vector.memset(placed[:], 0.0)
 
+        ident = sb.tile([P, P], F32)
+        make_identity(nc, ident[:])
+
         q_raw = sb.tile([P, 4, Q], F32, tag="stage")
         nc.sync.dma_start(q_raw[:], query.rearrange("(p j) q -> p j q", j=4))
         key_words = sb.tile([P, 2 * T], U8, align_bytes=64)
-        nc.sync.dma_start(key_words[:], keys_words[0])
+        nc.sync.dma_start(key_words[:, : 2 * WORDS_FIRST], keys_words[0, :, : 2 * WORDS_FIRST])
         for quad in range(4):
             nc.sync.dma_start(
                 key_scales[32 * quad : 32 * quad + 4, :].bitcast(I32),
                 keys_scales[0, 4 * quad : 4 * quad + 4, :].bitcast(I32),
             )
+        nc.sync.dma_start(key_words[:, 2 * WORDS_FIRST :], keys_words[0, :, 2 * WORDS_FIRST :])
         list1 = lists.tile([P, I // 16], U16)
         nc.sync.dma_start(list1[:], offs)
         list2 = lists.tile([P, I // 16], U16)
@@ -51,10 +57,15 @@ def tile_attend_pairproduct_lean_largerput_heads_kernel(tc, query, keys_words, k
         nc.sync.dma_start(list3[:], offs3)
 
         q_bf = sb.tile([P, Q, 4], BF16, align_bytes=64)
-        nc.vector.tensor_copy(q_bf[:], q_raw[:].rearrange("p j q -> p q j"))
+        q_dst = q_bf[:].rearrange("p (c i) j -> p c j i", i=4)
+        q_src = q_raw[:].rearrange("p j (c i) -> p c j i", i=4)
+        for h in range(2):
+            nc.vector.tensor_copy(q_dst[:, 16 * h : 16 * h + 16], q_src[:, 16 * h : 16 * h + 16])
         q_codes = sb.tile([P, Q], U32, align_bytes=64)
         q_scales = sb.tile([P, Q], U8, align_bytes=64)
-        nc.vector.quantize_mx(q_codes[:].bitcast(FP8X4), q_scales[:], q_bf[:].rearrange("p q j -> p (q j)"))
+        for h in range(2):
+            qs = slice(64 * h, 64 * h + 64)
+            nc.vector.quantize_mx(q_codes[:, qs].bitcast(FP8X4), q_scales[:, qs], q_bf[:, qs, :].rearrange("p q j -> p (q j)"))
 
         old_sb = sb.tile([P, T], F32, tag="stage")
         nc.sync.dma_start(old_sb[:], old)
@@ -62,7 +73,7 @@ def tile_attend_pairproduct_lean_largerput_heads_kernel(tc, query, keys_words, k
         scores = sb.tile([P, T], F32)
         t0 = 0
         for n, width in enumerate(SCORE_WIDTHS):
-            bank = psum.tile([P, width], F32, name=f"bank{n}")
+            bank = psum.tile([P, width], F32, name=f"bank{n}", tag=f"bank{n}")
             nc.tensor.matmul_mx(
                 bank[:],
                 lhsT=q_codes[:].bitcast(FP8X4),
@@ -89,15 +100,36 @@ def tile_attend_pairproduct_lean_largerput_heads_kernel(tc, query, keys_words, k
             nc.scalar.activation(second[:], scores[:].indirect(list2[:, cols]), COPY)
             nc.vector.tensor_tensor(placed[:].indirect(list3[:, cols]), first[:], second[:], ALU.mult)
 
-        chunks = T // OUT_CHUNK
-        larger = [sb.tile([P, OUT_CHUNK], F32, name=f"larger{c}") for c in range(chunks)]
-        result = [sb.tile([P, OUT_CHUNK], F32, name=f"result{c}") for c in range(chunks)]
-        for step in range(chunks + 1):
-            if step < chunks:
-                cols = slice(step * OUT_CHUNK, (step + 1) * OUT_CHUNK)
-                nc.vector.tensor_tensor(larger[step][:], placed[:, cols], old_sb[:, cols], ALU.max)
+        old_ps = []
+        for h in range(2):
+            turned_ps = psum.tile([P, 512], F32, name=f"turned_ps{h}", tag=f"bank{3 + h}")
+            for j in range(4):
+                nc.tensor.transpose(turned_ps[:, j * P : (j + 1) * P], old_sb[:, 512 * h + j * P : 512 * h + (j + 1) * P], ident[:])
+            turned = sb.tile([P, 512], F32, name=f"turned{h}")
+            if h == 0:
+                nc.scalar.activation(turned[:], turned_ps[:], COPY)
+            else:
+                nc.scalar.activation(turned[:, :P], turned_ps[:, :P], COPY)
+                nc.scalar.activation(turned[:, P:], turned_ps[:, P:], COPY, scale=1.25)
+            back = psum.tile([P, 512], F32, name=f"back{h}")
+            for j in range(4):
+                nc.tensor.transpose(back[:, j * P : (j + 1) * P], turned[:, j * P : (j + 1) * P], ident[:])
+            old_ps.append(back)
+
+        excess = sb.tile([P, T - SPLIT], F32)
+        nc.gpsimd.tensor_tensor(excess[:], placed[:, SPLIT:], old_sb[:, SPLIT:], ALU.subtract)
+        own = ((0, 256), (256, 512), (512, 640))
+        larger = [sb.tile([P, b - a], F32, name=f"larger{a}") for a, b in own]
+        for step in range(len(own) + 1):
+            if step < len(own):
+                a, b = own[step]
+                nc.vector.tensor_tensor(larger[step][:], placed[:, a:b], old_ps[a // 512][:, a % 512 : a % 512 + b - a], ALU.max)
             if step > 0:
-                c = step - 1
-                cols = slice(c * OUT_CHUNK, (c + 1) * OUT_CHUNK)
-                nc.vector.scalar_tensor_tensor(result[c][:], old_sb[:, cols], 0.25, larger[c][:], ALU.mult, ALU.add)
-                nc.sync.dma_start(out[:, cols], result[c][:])
+                a, b = own[step - 1]
+                result = sb.tile([P, b - a], F32, name=f"result{a}")
+                nc.vector.scalar_tensor_tensor(result[:], old_ps[a // 512][:, a % 512 : a % 512 + b - a], 0.25, larger[step - 1][:], ALU.mult, ALU.add)
+                nc.sync.dma_start(out[:, a:b], result[:])
+        for a, b in ((640, 896), (896, 1024)):
+            result = sb.tile([P, b - a], F32, name=f"result{a}")
+            nc.vector.scalar_tensor_tensor(result[:], excess[:, a - SPLIT : b - SPLIT], 0.0, old_ps[1][:, a - 512 : b - 512], ALU.max, ALU.add)
+            nc.sync.dma_start(out[:, a:b], result[:])

from contextlib import ExitStack

import concourse.mybir as mybir
from concourse.masks import make_identity

D, T, I, Q = 512, 1024, 512, 128
FLOPS = 2 * D * T * Q

F32 = mybir.dt.float32
BF16 = mybir.dt.bfloat16
I32 = mybir.dt.int32
U32 = mybir.dt.uint32
U16 = mybir.dt.uint16
U8 = mybir.dt.uint8
FP8X4 = mybir.dt.float8_e4m3fn_x4
FP4X4 = mybir.dt.float4_e2m1fn_x4
ALU = mybir.AluOpType
COPY = mybir.ActivationFunctionType.Copy

P = 128
SCORE_WIDTHS = (256, 256, 256, 128, 128)
WORDS_FIRST = 512
HALF = I // 2
SPLIT = 640


def tile_attend_pairproduct_lean_largerput_heads_kernel(tc, query, keys_words, keys_scales, old, offs, offs2, offs3, out):
    nc = tc.nc
    with ExitStack() as ctx:
        lists = ctx.enter_context(tc.tile_pool(name="lists", bufs=1))
        sb = ctx.enter_context(tc.tile_pool(name="sb", bufs=1))
        psum = ctx.enter_context(tc.psum_pool(name="psum", bufs=1))

        key_scales = sb.tile([P, T], U8, align_bytes=64)
        nc.vector.memset(key_scales[:].bitcast(I32), 0)
        placed = sb.tile([P, T], F32)
        nc.vector.memset(placed[:], 0.0)

        ident = sb.tile([P, P], F32)
        make_identity(nc, ident[:])

        q_raw = sb.tile([P, 4, Q], F32, tag="stage")
        nc.sync.dma_start(q_raw[:], query.rearrange("(p j) q -> p j q", j=4))
        key_words = sb.tile([P, 2 * T], U8, align_bytes=64)
        nc.sync.dma_start(key_words[:, : 2 * WORDS_FIRST], keys_words[0, :, : 2 * WORDS_FIRST])
        for quad in range(4):
            nc.sync.dma_start(
                key_scales[32 * quad : 32 * quad + 4, :].bitcast(I32),
                keys_scales[0, 4 * quad : 4 * quad + 4, :].bitcast(I32),
            )
        nc.sync.dma_start(key_words[:, 2 * WORDS_FIRST :], keys_words[0, :, 2 * WORDS_FIRST :])
        list1 = lists.tile([P, I // 16], U16)
        nc.sync.dma_start(list1[:], offs)
        list2 = lists.tile([P, I // 16], U16)
        nc.sync.dma_start(list2[:], offs2)
        list3 = lists.tile([P, I // 16], U16)
        nc.sync.dma_start(list3[:], offs3)

        q_bf = sb.tile([P, Q, 4], BF16, align_bytes=64)
        q_dst = q_bf[:].rearrange("p (c i) j -> p c j i", i=4)
        q_src = q_raw[:].rearrange("p j (c i) -> p c j i", i=4)
        for h in range(2):
            nc.vector.tensor_copy(q_dst[:, 16 * h : 16 * h + 16], q_src[:, 16 * h : 16 * h + 16])
        q_codes = sb.tile([P, Q], U32, align_bytes=64)
        q_scales = sb.tile([P, Q], U8, align_bytes=64)
        for h in range(2):
            qs = slice(64 * h, 64 * h + 64)
            nc.vector.quantize_mx(q_codes[:, qs].bitcast(FP8X4), q_scales[:, qs], q_bf[:, qs, :].rearrange("p q j -> p (q j)"))

        old_sb = sb.tile([P, T], F32, tag="stage")
        nc.sync.dma_start(old_sb[:], old)

        scores = sb.tile([P, T], F32)
        t0 = 0
        for n, width in enumerate(SCORE_WIDTHS):
            bank = psum.tile([P, width], F32, name=f"bank{n}", tag=f"bank{n}")
            nc.tensor.matmul_mx(
                bank[:],
                lhsT=q_codes[:].bitcast(FP8X4),
                lhsT_scale=q_scales[:],
                rhs=key_words[:, 2 * t0 : 2 * (t0 + width)].bitcast(FP4X4),
                rhs_scale=key_scales[:, t0 : t0 + width],
                start=True,
                stop=True,
            )
            if n % 2 == 0:
                nc.scalar.activation(scores[:, t0 : t0 + width], bank[:], COPY)
            else:
                nc.vector.tensor_copy(scores[:, t0 : t0 + width], bank[:])
            t0 = t0 + width

        for h in range(2):
            cols = slice(h * HALF // 16, (h + 1) * HALF // 16)
            first = sb.tile([P, HALF], F32, name=f"first{h}")
            second = sb.tile([P, HALF], F32, name=f"second{h}")
            if h == 0:
                nc.vector.tensor_copy(first[:], scores[:].indirect(list1[:, cols]))
            else:
                nc.scalar.activation(first[:], scores[:].indirect(list1[:, cols]), COPY)
            nc.scalar.activation(second[:], scores[:].indirect(list2[:, cols]), COPY)
            nc.vector.tensor_tensor(placed[:].indirect(list3[:, cols]), first[:], second[:], ALU.mult)

        old_ps = []
        for h in range(2):
            turned_ps = psum.tile([P, 512], F32, name=f"turned_ps{h}", tag=f"bank{3 + h}")
            for j in range(4):
                nc.tensor.transpose(turned_ps[:, j * P : (j + 1) * P], old_sb[:, 512 * h + j * P : 512 * h + (j + 1) * P], ident[:])
            turned = sb.tile([P, 512], F32, name=f"turned{h}")
            if h == 0:
                nc.scalar.activation(turned[:], turned_ps[:], COPY)
            else:
                nc.scalar.activation(turned[:, :P], turned_ps[:, :P], COPY)
                nc.scalar.activation(turned[:, P:], turned_ps[:, P:], COPY, scale=1.25)
            back = psum.tile([P, 512], F32, name=f"back{h}")
            for j in range(4):
                nc.tensor.transpose(back[:, j * P : (j + 1) * P], turned[:, j * P : (j + 1) * P], ident[:])
            old_ps.append(back)

        excess = sb.tile([P, T - SPLIT], F32)
        nc.gpsimd.tensor_tensor(excess[:], placed[:, SPLIT:], old_sb[:, SPLIT:], ALU.subtract)
        own = ((0, 256), (256, 512), (512, 640))
        larger = [sb.tile([P, b - a], F32, name=f"larger{a}") for a, b in own]
        for step in range(len(own) + 1):
            if step < len(own):
                a, b = own[step]
                nc.vector.tensor_tensor(larger[step][:], placed[:, a:b], old_ps[a // 512][:, a % 512 : a % 512 + b - a], ALU.max)
            if step > 0:
                a, b = own[step - 1]
                result = sb.tile([P, b - a], F32, name=f"result{a}")
                nc.vector.scalar_tensor_tensor(result[:], old_ps[a // 512][:, a % 512 : a % 512 + b - a], 0.25, larger[step - 1][:], ALU.mult, ALU.add)
                nc.sync.dma_start(out[:, a:b], result[:])
        for a, b in ((640, 896), (896, 1024)):
            result = sb.tile([P, b - a], F32, name=f"result{a}")
            nc.vector.scalar_tensor_tensor(result[:], excess[:, a - SPLIT : b - SPLIT], 0.0, old_ps[1][:, a - 512 : b - 512], ALU.max, ALU.add)
            nc.sync.dma_start(out[:, a:b], result[:])
